import numpy as np
import ml_dtypes


def mxq(x, axis, fmt="e4m3"):
    dtype, down = {"e4m3": (ml_dtypes.float8_e4m3fn, 7), "e5m2": (ml_dtypes.float8_e5m2, 14)}[fmt]
    v = np.moveaxis(np.asarray(x, np.float32).astype(ml_dtypes.bfloat16).astype(np.float64), axis, -1)
    blocks = v.reshape(v.shape[:-1] + (-1, 32))
    amax = np.abs(blocks).max(-1, keepdims=True)
    byte = np.maximum(np.where(amax > 0, np.frexp(amax)[1] - 1 + 127, 0) - down, 1)
    scale = np.exp2(byte - 127.0)
    codes = (blocks / scale).astype(np.float32).astype(dtype).astype(np.float64)
    return np.moveaxis((codes * scale).reshape(v.shape), -1, axis)


WIDE = False


def mx_kscale(k):
    if not WIDE:
        return np.ones(k)
    levels = np.array([10, -10, 5, -5, 0])
    if k % 512:
        return np.exp2(np.random.permutation(np.resize(levels, k // 32))).repeat(32)
    a = np.empty((k // 512, 16))
    for p in range(k // 512):
        a[p, :8] = np.random.permutation(np.resize(levels, 8))
        for g in range(8):
            far = levels[np.abs(levels - a[p, g]) >= 10]
            a[p, g + 8] = far[np.random.randint(len(far))]
    return np.exp2(a.ravel()).repeat(32)


def f64(x):
    return np.asarray(x).astype(np.float64)


def striped(idx):
    return np.tile(idx.reshape(-1, 16).T, (8, 1)).astype(np.uint16)


def unstriped(offs):
    return offs[:16].T.reshape(-1).astype(np.int64)


E2M1 = np.array([0.0, 0.5, 1.0, 1.5, 2.0, 3.0, 4.0, 6.0, -0.0, -0.5, -1.0, -1.5, -2.0, -3.0, -4.0, -6.0])


def pack_weight(w, fmt):
    k, n = w.shape
    w = f64(np.asarray(w, np.float32).astype(ml_dtypes.bfloat16)).reshape(k // 32, 32, n)
    amax = np.abs(w).max(1)
    if fmt == "e4m3":
        byte = np.frexp(amax)[1] - 1 + 127 - 7
    else:
        mant, ex = np.frexp(amax / 6.0)
        byte = np.where(mant > 0.5, ex, ex - 1) + 127
    byte = np.clip(np.where(amax > 0, byte, 1), 1, 254)
    scaled = (w * np.exp2(127.0 - byte)[:, None, :]).reshape(k, n).astype(np.float32)
    by_word = np.ascontiguousarray(scaled.reshape(k // 512, 128, 4, n).transpose(0, 1, 3, 2))
    if fmt == "e4m3":
        words = by_word.astype(ml_dtypes.float8_e4m3fn).view(np.uint8)
    else:
        c = by_word.astype(ml_dtypes.float4_e2m1fn).view(np.uint8) & 0xF
        words = (c[..., 0::2] | (c[..., 1::2] << 4)).reshape(k // 512, 128, 2 * n)
    return np.ascontiguousarray(words), np.ascontiguousarray(byte.astype(np.uint8).reshape(k // 512, 16, n))


def unpack_weight(words, scales, fmt):
    g, _, n = scales.shape
    words = np.ascontiguousarray(words).reshape(g, 128, n, -1)
    if fmt == "e4m3":
        vals = words.view(ml_dtypes.float8_e4m3fn).astype(np.float64)
    else:
        nib = np.empty((g, 128, n, 4), np.uint8)
        nib[..., 0::2] = words & 0xF
        nib[..., 1::2] = words >> 4
        vals = E2M1[nib]
    vals = vals * np.repeat(np.exp2(scales.astype(np.float64) - 127.0), 8, axis=1)[..., None]
    return vals.transpose(0, 1, 3, 2).reshape(g * 512, n)


def gelu(v):
    return 0.5 * v * (1.0 + np.tanh(np.sqrt(2.0 / np.pi) * (v + 0.044715 * v**3)))


def bf(x):
    return np.asarray(x, np.float32).astype(ml_dtypes.bfloat16)


def planes(Y):
    n, m = Y.shape
    b = f64(bf(Y)).reshape(n // 32, 32, m)
    amax = np.abs(b).max(1)
    byte = np.clip(np.where(amax > 0, np.frexp(amax)[1] - 1 + 127 - 7, 1), 1, 254)
    codes = (b * np.exp2(127.0 - byte)[:, None, :]).reshape(n, m).astype(np.float32).astype(ml_dtypes.float8_e4m3fn).view(np.uint8)
    words = codes.reshape(n // 512, 128, 4, m).transpose(0, 1, 3, 2)
    return np.ascontiguousarray(words), np.ascontiguousarray(byte.astype(np.uint8).reshape(n // 512, 16, m))


K, T, S, T2, P, H, N = 1024, 4096, 1024, 2048, 1024, 512, 1024

def setup_inputs():
    n = np.random.standard_normal
    s = mx_kscale(K)[:, None]
    u = mx_kscale(H)[:, None]
    tab_words, tab_scales = pack_weight(n((K, T)) * s, "e4m3")
    w2_words, w2_scales = pack_weight(n((K, H)) / np.sqrt(K) / s * u.T, "e2m1")
    w4_words, w4_scales = pack_weight(n((H, N)) / np.sqrt(H) / u * np.exp(0.8 * n(N)), "e2m1")
    return {
        "tab_words": tab_words, "tab_scales": tab_scales,
        "offs": striped(np.random.permutation(T)[:S]),
        "offs2": striped(np.random.permutation(T2)[:S]),
        "offs3": striped(np.random.permutation(T2)[:P]),
        "offs4": striped(np.random.permutation(T2)[:P]),
        "w1": (n((K, H)) / np.sqrt(K) / s * u.T).astype(np.float32),
        "w2_words": w2_words, "w2_scales": w2_scales,
        "w3": (n((K, H)) / np.sqrt(K) / s * u.T).astype(np.float32),
        "wgs": np.exp(0.3 * n((128, S))).astype(np.float32),
        "page0": (n((H, T2)) * u).astype(np.float32),
        "shift": (0.8 * n(H) * u[:, 0]).astype(np.float32),
        "w4_words": w4_words, "w4_scales": w4_scales,
    }

def reference(tab_words, tab_scales, offs, offs2, offs3, offs4, w1, w2_words, w2_scales, w3, wgs, page0, shift, w4_words, w4_scales):
    v = unpack_weight(tab_words, tab_scales, "e4m3")[:, unstriped(offs)]
    a1 = mxq(f64(w1), 0, "e4m3").T @ v
    a2 = unpack_weight(w2_words, w2_scales, "e2m1").T @ v
    a3 = mxq(f64(w3), 0, "e4m3").T @ v
    h = np.minimum(np.maximum(a1, a2), a3)
    before = f64(page0)
    page = before.copy()
    page[:, unstriped(offs2)] = np.tile(f64(wgs), (H // 128, 1)) * h
    x = page[:, unstriped(offs3)] + f64(shift)[:, None]
    x = x - before[:, unstriped(offs4)]
    y = unpack_weight(w4_words, w4_scales, "e2m1").T @ mxq(x, 0, "e4m3")
    words, scales = planes(y)
    return y, words, scales

@@ -1,0 +1,296 @@
+from contextlib import ExitStack
+
+import concourse.mybir as mybir
+
+K, T, S, T2, M, H, N = 1024, 4096, 1024, 2048, 1024, 512, 1024
+FLOPS = 2 * (3 * K * H * S + H * N * M)
+
+F32 = mybir.dt.float32
+BF16 = mybir.dt.bfloat16
+I32 = mybir.dt.int32
+U32 = mybir.dt.uint32
+U16 = mybir.dt.uint16
+U8 = mybir.dt.uint8
+FP8X4 = mybir.dt.float8_e4m3fn_x4
+FP4X4 = mybir.dt.float4_e2m1fn_x4
+ALU = mybir.AluOpType
+ACT = mybir.ActivationFunctionType
+
+P = 128
+PACK = 4
+QUADS = 4
+PASSES = K // (P * PACK)
+GROUPS = N // (P * PACK)
+BANK = 512
+HALVES = S // BANK
+EDGES = (0, 128, 384, 640, 896, 1024)
+BLOCK = 128
+
+
+def tile_list_free_span_features_kernel(
+    tc, tab_words, tab_scales, offs, offs2, offs3, offs4, w1, w2_words, w2_scales, w3, wgs, page0, shift,
+    w4_words, w4_scales, out_0, out_1, out_2,
+):
+    nc = tc.nc
+    with ExitStack() as ctx:
+        lists = ctx.enter_context(tc.tile_pool(name="lists", bufs=1))
+        keep = ctx.enter_context(tc.tile_pool(name="keep", bufs=1))
+        ring = ctx.enter_context(tc.tile_pool(name="ring", bufs=2))
+        psum = ctx.enter_context(tc.psum_pool(name="psum", bufs=8))
+
+        idx = lists.tile([P, S // 16], U16, name="idx")
+        idx2 = lists.tile([P, S // 16], U16, name="idx2")
+        idx3 = lists.tile([P, M // 16], U16, name="idx3")
+        idx4 = lists.tile([P, M // 16], U16, name="idx4")
+
+        tab_w = [keep.tile([P, T], I32, name=f"tab_w{a}", tag=f"big{a}", align_bytes=64) for a in range(PASSES)]
+        tab_s = keep.tile([P, T], U8, name="tab_s")
+        page = [keep.tile([P, T2], F32, name=f"page{t}") for t in range(PACK)]
+        gain = keep.tile([P, PACK, S], F32, name="gain", tag="gain")
+        w_raw = [[keep.tile([P, PACK, H], F32, name=f"w_raw{i}{a}") for a in range(PASSES)] for i in range(2)]
+        w2_raw = keep.tile([P, PASSES, 2 * H], U8, name="w2_raw")
+        w2_sraw = keep.tile([P, PASSES, H], U8, name="w2_sraw")
+        w4_raw = keep.tile([P, 2 * N], U8, name="w4_raw")
+        w4_sraw = keep.tile([P, N], U8, name="w4_sraw")
+        shift_t = keep.tile([P, PACK], F32, name="shift_t")
+        v_s1 = keep.tile([P, S], U8, name="v_s1", align_bytes=64)
+
+        page_rows = page0.rearrange("(p t) c -> t p c", t=PACK)
+        gain_rows = wgs.rearrange("(p t) j -> p t j", t=PACK)
+
+        def load_w(i, w, a):
+            rows = w[a * P * PACK : (a + 1) * P * PACK, :]
+            nc.sync.dma_start(out=w_raw[i][a][:], in_=rows.rearrange("(p j) c -> p j c", j=PACK))
+
+        def load_tab(a):
+            nc.sync.dma_start(out=tab_w[a][:], in_=tab_words[a].rearrange("p c i -> p (c i)").bitcast(I32))
+
+        nc.vector.memset(tab_s[:].bitcast(I32), 0)
+        nc.vector.memset(w2_sraw[:].rearrange("p a c -> p (a c)").bitcast(I32), 0)
+        nc.vector.memset(v_s1[:].bitcast(I32), 0)
+        nc.vector.memset(w4_sraw[:].bitcast(I32), 0)
+
+        def load_page(t):
+            nc.sync.dma_start(out=page[t][:], in_=page_rows[t])
+
+        def load_w2_scales(q):
+            nc.sync.dma_start(
+                out=w2_sraw[32 * q : 32 * q + 4, :, :].bitcast(I32),
+                in_=w2_scales[:, 4 * q : 4 * q + 4, :].rearrange("a r c -> r a c").bitcast(I32),
+            )
+
+        nc.sync.dma_start(idx4[:], offs4)
+        load_page(0)
+        nc.sync.dma_start(idx[:], offs)
+        nc.sync.dma_start(out=shift_t[:], in_=shift.rearrange("(p t) -> p t", t=PACK))
+        nc.sync.dma_start(idx2[:], offs2)
+        nc.sync.dma_start(idx3[:], offs3)
+        nc.sync.dma_start(out=w2_raw[:].bitcast(I32), in_=w2_words.rearrange("a p c -> p a c").bitcast(I32))
+        load_page(1)
+        for q in range(QUADS):
+            nc.sync.dma_start(
+                out=tab_s[32 * q : 32 * q + 4 * PASSES, :].bitcast(I32),
+                in_=tab_scales[:, 4 * q : 4 * q + 4, :].bitcast(I32),
+            )
+        load_tab(0)
+        for q in range(QUADS):
+            load_w2_scales(q)
+        load_tab(1)
+        for a in range(PASSES):
+            load_w(0, w1, a)
+        load_page(2)
+        for a in range(PASSES):
+            load_w(1, w3, a)
+        load_page(3)
+        for q in range(QUADS):
+            nc.sync.dma_start(out=gain[32 * q : 32 * q + 32, 0, :], in_=gain_rows[:, 0, :])
+        for q in range(QUADS):
+            nc.sync.dma_start(out=gain[32 * q : 32 * q + 32, 1:PACK, :], in_=gain_rows[:, 1:PACK, :])
+        nc.sync.dma_start(out=w4_raw[:].bitcast(I32), in_=w4_words[0].bitcast(I32))
+        for q in range(QUADS):
+            nc.sync.dma_start(
+                out=w4_sraw[32 * q : 32 * q + 4, :].bitcast(I32),
+                in_=w4_scales[0, 4 * q : 4 * q + 4, :].bitcast(I32),
+            )
+
+
+        v_s0 = keep.tile([P, S], U8, name="v_s0", align_bytes=64)
+        v_s = [v_s0, v_s1]
+
+        base = [keep.tile([P, M], F32, name=f"base{t}") for t in range(PACK)]
+
+        def before(t):
+            old = ring.tile([P, M], F32, name="old")
+            nc.vector.tensor_copy(old[:], page[t][:].indirect(idx4[:]))
+            nc.scalar.activation(base[t][:], old[:], ACT.Identity, bias=shift_t[:, t : t + 1], scale=-1.0)
+
+        v_w = [keep.tile([P, S], U32, name=f"v_w{a}", align_bytes=64) for a in range(PASSES)]
+
+        def pick(a):
+            nc.vector.tensor_copy(v_w[a][:], tab_w[a][:].bitcast(U32).indirect(idx[:]))
+
+        w2_c = keep.tile([P, PASSES, 2 * H], U8, name="w2_c", align_bytes=64)
+        w2_s = keep.tile([P, PASSES, H], U8, name="w2_s", align_bytes=64)
+        w4_c = keep.tile([P, GROUPS, 2 * BANK], U8, name="w4_c", align_bytes=64)
+        w4_s = keep.tile([P, GROUPS, BANK], U8, name="w4_s", align_bytes=64)
+
+        def deal(dst, src):
+            nc.vector.tensor_copy(
+                dst.rearrange("p a (t q) -> p a t q", t=PACK), src.rearrange("p a (q t) -> p a t q", t=PACK)
+            )
+
+        before(0)
+        deal(w2_c[:].bitcast(U16), w2_raw[:].bitcast(U16))
+        before(1)
+        nc.vector.tensor_copy(v_s0[:], tab_s[:].indirect(idx[:]))
+        nc.scalar.dma_start(out=v_s1[0:112, :].bitcast(I32), in_=v_s0[4:116, :].bitcast(I32))
+        pick(0)
+        deal(w2_s[:], w2_sraw[:])
+        pick(1)
+
+        w_c = [[keep.tile([P, H], U32, name=f"w_c{i}{a}", align_bytes=64) for a in range(PASSES)] for i in range(2)]
+        w_s = [[keep.tile([P, H], U8, name=f"w_s{i}{a}", align_bytes=64) for a in range(PASSES)] for i in range(2)]
+
+        def quantize_w(i, copy):
+            woven = []
+            for a in range(PASSES):
+                w_b = ring.tile([P, PACK * H], BF16, name="w_b", align_bytes=64)
+                copy(
+                    w_b[:].rearrange("p (t q j) -> p q j t", t=PACK, j=PACK),
+                    w_raw[i][a][:].rearrange("p j (q t) -> p q j t", t=PACK),
+                )
+                woven.append(w_b)
+            for a in range(PASSES):
+                nc.vector.quantize_mx(out=w_c[i][a][:].bitcast(FP8X4), scales=w_s[i][a][:], in_=woven[a][:])
+
+        h = [keep.tile([P, S], F32, name=f"h{t}") for t in range(PACK)]
+
+        def project(codes, scales, u):
+            acc = psum.tile([P, BANK], F32, name="acc")
+            cols = slice(u * BANK, (u + 1) * BANK)
+            for a in range(PASSES):
+                nc.tensor.matmul_mx(
+                    out=acc[:], lhsT=codes[a], lhsT_scale=scales[a],
+                    rhs=v_w[a][:, cols].bitcast(FP8X4), rhs_scale=v_s[a][:, cols],
+                    start=(a == 0), stop=(a == PASSES - 1),
+                )
+            return acc
+
+        def project_fp8(i, t, u):
+            rows = slice(t * P, (t + 1) * P)
+            return project(
+                [w_c[i][a][:, rows].bitcast(FP8X4) for a in range(PASSES)],
+                [w_s[i][a][:, rows] for a in range(PASSES)], u,
+            )
+
+        for t in range(PACK):
+            for u in range(HALVES):
+                acc = project(
+                    [w2_c[:, a, 2 * t * P : 2 * (t + 1) * P].bitcast(FP4X4) for a in range(PASSES)],
+                    [w2_s[:, a, t * P : (t + 1) * P] for a in range(PASSES)], u,
+                )
+                nc.scalar.copy(h[t][:, u * BANK : (u + 1) * BANK], acc[:])
+
+        quantize_w(0, nc.vector.tensor_copy)
+        before(2)
+        for t in range(PACK):
+            for u in range(HALVES):
+                acc = project_fp8(0, t, u)
+                part = h[t][:, u * BANK : (u + 1) * BANK]
+                nc.vector.tensor_tensor(part, acc[:], part, ALU.max)
+
+        quantize_w(1, nc.scalar.copy)
+        before(3)
+
+        def limit(t):
+            for u in range(HALVES):
+                acc = project_fp8(1, t, u)
+                part = h[t][:, u * BANK : (u + 1) * BANK]
+                nc.vector.tensor_tensor(part, acc[:], part, ALU.min)
+
+        def rewrite(t):
+            nc.vector.tensor_tensor(page[t][:].indirect(idx2[:]), h[t][:], gain[:, t, :], ALU.mult)
+
+        limit(0)
+        limit(1)
+        rewrite(0)
+        limit(2)
+        rewrite(1)
+        limit(3)
+        deal(w4_c[:].bitcast(U16), w4_raw[:].rearrange("p (g c) -> p g c", g=GROUPS).bitcast(U16))
+        deal(w4_s[:], w4_sraw[:].rearrange("p (g c) -> p g c", g=GROUPS))
+        rewrite(2)
+        rewrite(3)
+
+        x_f = keep.tile([P, PACK * M], F32, name="x_f", tag="gain")
+        y = [keep.tile([P, PACK, M], F32, name=f"y{g}", tag=f"big{g}", align_bytes=64) for g in range(GROUPS)]
+        y_c = keep.tile([P, GROUPS, M], I32, name="y_c", align_bytes=64)
+        y_s = keep.tile([P, GROUPS, M], U8, name="y_s", align_bytes=64)
+        y_rows = out_0.rearrange("(g p t) m -> g p t m", p=P, t=PACK)
+        y_words = out_1.rearrange("g p m t -> p g (m t)").bitcast(I32)
+
+        def weave(copy, dst, src):
+            copy(
+                dst.rearrange("p (c i t) -> p c t i", i=4, t=PACK),
+                src.rearrange("p t (c i) -> p c t i", i=4),
+            )
+
+        def fetch(m0, m1):
+            width = m1 - m0
+            part = idx3[:, m0 // 16 : m1 // 16]
+            x_part = x_f[:, PACK * m0 : PACK * m1].rearrange("p (t m) -> p t m", t=PACK)
+            for t in range(PACK):
+                nc.vector.tensor_tensor(x_part[:, t, :], page[t][:].indirect(part), base[t][:, m0:m1], ALU.add)
+            x_b = ring.tile([P, PACK * width], BF16, name="x_b", align_bytes=64)
+            weave(nc.scalar.copy, x_b[:], x_part)
+            return x_b
+
+        def multiply(m0, m1, x_b):
+            width = m1 - m0
+            x_c = ring.tile([P, width], U32, name="x_c", align_bytes=64)
+            x_s = ring.tile([P, width], U8, name="x_s", align_bytes=64)
+            nc.vector.quantize_mx(out=x_c[:].bitcast(FP8X4), scales=x_s[:], in_=x_b[:])
+            for g in range(GROUPS):
+                for b0 in range(0, width, BLOCK):
+                    acc = psum.tile([P, BANK], F32, name="acc")
+                    cols = slice(b0, b0 + BLOCK)
+                    for t in range(PACK):
+                        nc.tensor.matmul_mx(
+                            out=acc[:, t * BLOCK : (t + 1) * BLOCK],
+                            lhsT=w4_c[:, g, 2 * t * P : 2 * (t + 1) * P].bitcast(FP4X4),
+                            lhsT_scale=w4_s[:, g, t * P : (t + 1) * P],
+                            rhs=x_c[:, cols].bitcast(FP8X4), rhs_scale=x_s[:, cols],
+                            start=True, stop=True,
+                        )
+                    nc.scalar.copy(
+                        y[g][:, :, m0 + b0 : m0 + b0 + BLOCK], acc[:].rearrange("p (t m) -> p t m", t=PACK)
+                    )
+
+        def finish(m0, m1):
+            cols = slice(m0, m1)
+            woven = []
+            for g in range(GROUPS):
+                nc.sync.dma_start(out=y_rows[g][:, :, cols], in_=y[g][:, :, cols])
+                y_b = ring.tile([P, PACK * (m1 - m0)], BF16, name="y_b", align_bytes=64)
+                weave(nc.vector.tensor_copy, y_b[:], y[g][:, :, cols])
+                woven.append(y_b)
+            for g in range(GROUPS):
+                nc.vector.quantize_mx(out=y_c[:, g, cols].bitcast(FP8X4), scales=y_s[:, g, cols], in_=woven[g][:])
+            nc.sync.dma_start(out=y_words[:, :, cols], in_=y_c[:, :, cols])
+
+        spans = list(zip(EDGES[:-1], EDGES[1:]))
+        x_next = fetch(*spans[0])
+        for c, span in enumerate(spans):
+            x_b = x_next
+            if c + 1 < len(spans):
+                x_next = fetch(*spans[c + 1])
+            multiply(*span, x_b)
+            if c > 0:
+                finish(*spans[c - 1])
+        finish(*spans[-1])
+
+        for q in range(QUADS):
+            nc.scalar.dma_start(
+                out=out_2[:, 4 * q : 4 * q + 4, :].rearrange("g r m -> r g m").bitcast(I32),
+                in_=y_s[32 * q : 32 * q + 4, :, :].bitcast(I32),
+            )

@@ -156,8 +156,8 @@ def tile_list_free_span_features_kernel(
             for a in range(PASSES):
                 w_b = ring.tile([P, PACK * H], BF16, name="w_b", align_bytes=64)
                 copy(
-                    w_b[:].rearrange("p (t q j) -> p q j t", t=PACK, j=PACK),
-                    w_raw[i][a][:].rearrange("p j (q t) -> p q j t", t=PACK),
+                    w_b[:].rearrange("p (t q j) -> p q t j", t=PACK, j=PACK),
+                    w_raw[i][a][:].rearrange("p j (q t) -> p q t j", t=PACK),
                 )
                 woven.append(w_b)
             for a in range(PASSES):
@@ -266,13 +266,13 @@ def tile_list_free_span_features_kernel(
                         y[g][:, :, m0 + b0 : m0 + b0 + BLOCK], acc[:].rearrange("p (t m) -> p t m", t=PACK)
                     )
 
-        def finish(m0, m1):
+        def finish(m0, m1, copy):
             cols = slice(m0, m1)
             woven = []
             for g in range(GROUPS):
                 nc.sync.dma_start(out=y_rows[g][:, :, cols], in_=y[g][:, :, cols])
-                y_b = ring.tile([P, PACK * (m1 - m0)], BF16, name="y_b", align_bytes=64)
-                weave(nc.vector.tensor_copy, y_b[:], y[g][:, :, cols])
+                y_b = ring.tile([P, PACK * (m1 - m0)], BF16, name="y_b", bufs=4, align_bytes=64)
+                weave(copy, y_b[:], y[g][:, :, cols])
                 woven.append(y_b)
             for g in range(GROUPS):
                 nc.vector.quantize_mx(out=y_c[:, g, cols].bitcast(FP8X4), scales=y_s[:, g, cols], in_=woven[g][:])
@@ -285,9 +285,10 @@ def tile_list_free_span_features_kernel(
             if c + 1 < len(spans):
                 x_next = fetch(*spans[c + 1])
             multiply(*span, x_b)
-            if c > 0:
-                finish(*spans[c - 1])
-        finish(*spans[-1])
+            if c == 0:
+                finish(*span, nc.scalar.copy)
+        for span in spans[1:]:
+            finish(*span, nc.vector.tensor_copy)
 
         for q in range(QUADS):
             nc.scalar.dma_start(

@@ -18,13 +18,14 @@ ACT = mybir.ActivationFunctionType
 
 P = 128
 PACK = 4
-QUADS = 4
 PASSES = K // (P * PACK)
 GROUPS = N // (P * PACK)
 BANK = 512
 HALVES = S // BANK
 EDGES = (0, 128, 384, 640, 896, 1024)
 BLOCK = 128
+BANKS = 8
+QUAD_ORDER = (0, 2, 1, 3)
 
 
 def tile_list_free_span_features_kernel(
@@ -36,7 +37,7 @@ def tile_list_free_span_features_kernel(
         lists = ctx.enter_context(tc.tile_pool(name="lists", bufs=1))
         keep = ctx.enter_context(tc.tile_pool(name="keep", bufs=1))
         ring = ctx.enter_context(tc.tile_pool(name="ring", bufs=2))
-        psum = ctx.enter_context(tc.psum_pool(name="psum", bufs=8))
+        psum = ctx.enter_context(tc.psum_pool(name="psum", bufs=1))
 
         idx = lists.tile([P, S // 16], U16, name="idx")
         idx2 = lists.tile([P, S // 16], U16, name="idx2")
@@ -65,10 +66,10 @@ def tile_list_free_span_features_kernel(
         def load_tab(a):
             nc.sync.dma_start(out=tab_w[a][:], in_=tab_words[a].rearrange("p c i -> p (c i)").bitcast(I32))
 
-        nc.vector.memset(tab_s[:].bitcast(I32), 0)
         nc.vector.memset(w2_sraw[:].rearrange("p a c -> p (a c)").bitcast(I32), 0)
-        nc.vector.memset(v_s1[:].bitcast(I32), 0)
+        nc.vector.memset(tab_s[:].bitcast(I32), 0)
         nc.vector.memset(w4_sraw[:].bitcast(I32), 0)
+        nc.vector.memset(v_s1[:].bitcast(I32), 0)
 
         def load_page(t):
             nc.sync.dma_start(out=page[t][:], in_=page_rows[t])
@@ -79,40 +80,37 @@ def tile_list_free_span_features_kernel(
                 in_=w2_scales[:, 4 * q : 4 * q + 4, :].rearrange("a r c -> r a c").bitcast(I32),
             )
 
+        nc.sync.dma_start(out=w2_raw[:].bitcast(I32), in_=w2_words.rearrange("a p c -> p a c").bitcast(I32))
+        nc.sync.dma_start(out=w4_raw[:].bitcast(I32), in_=w4_words[0].bitcast(I32))
         nc.sync.dma_start(idx4[:], offs4)
-        load_page(0)
         nc.sync.dma_start(idx[:], offs)
         nc.sync.dma_start(out=shift_t[:], in_=shift.rearrange("(p t) -> p t", t=PACK))
         nc.sync.dma_start(idx2[:], offs2)
         nc.sync.dma_start(idx3[:], offs3)
-        nc.sync.dma_start(out=w2_raw[:].bitcast(I32), in_=w2_words.rearrange("a p c -> p a c").bitcast(I32))
-        load_page(1)
-        for q in range(QUADS):
-            nc.sync.dma_start(
-                out=tab_s[32 * q : 32 * q + 4 * PASSES, :].bitcast(I32),
-                in_=tab_scales[:, 4 * q : 4 * q + 4, :].bitcast(I32),
-            )
-        load_tab(0)
-        for q in range(QUADS):
+        load_page(0)
+        for q in QUAD_ORDER:
             load_w2_scales(q)
-        load_tab(1)
-        for a in range(PASSES):
-            load_w(0, w1, a)
-        load_page(2)
-        for a in range(PASSES):
-            load_w(1, w3, a)
-        load_page(3)
-        for q in range(QUADS):
-            nc.sync.dma_start(out=gain[32 * q : 32 * q + 32, 0, :], in_=gain_rows[:, 0, :])
-        for q in range(QUADS):
-            nc.sync.dma_start(out=gain[32 * q : 32 * q + 32, 1:PACK, :], in_=gain_rows[:, 1:PACK, :])
-        nc.sync.dma_start(out=w4_raw[:].bitcast(I32), in_=w4_words[0].bitcast(I32))
-        for q in range(QUADS):
+        load_page(1)
+        tab_rows = tab_scales.rearrange("a (q r) c -> r q a c", r=4).bitcast(I32)
+        for r in range(4):
+            nc.sync.dma_start(out=tab_s[r:P:16, :].bitcast(I32), in_=tab_rows[r])
+        load_tab(0)
+        for q in QUAD_ORDER:
             nc.sync.dma_start(
                 out=w4_sraw[32 * q : 32 * q + 4, :].bitcast(I32),
                 in_=w4_scales[0, 4 * q : 4 * q + 4, :].bitcast(I32),
             )
-
+        for a in range(PASSES):
+            load_w(0, w1, a)
+        load_tab(1)
+        load_page(2)
+        for a in range(PASSES):
+            load_w(1, w3, a)
+        load_page(3)
+        for q in QUAD_ORDER:
+            nc.sync.dma_start(out=gain[32 * q : 32 * q + 32, 0, :], in_=gain_rows[:, 0, :])
+        for q in QUAD_ORDER:
+            nc.sync.dma_start(out=gain[32 * q : 32 * q + 32, 1:PACK, :], in_=gain_rows[:, 1:PACK, :])
 
         v_s0 = keep.tile([P, S], U8, name="v_s0", align_bytes=64)
         v_s = [v_s0, v_s1]
@@ -139,15 +137,6 @@ def tile_list_free_span_features_kernel(
                 dst.rearrange("p a (t q) -> p a t q", t=PACK), src.rearrange("p a (q t) -> p a t q", t=PACK)
             )
 
-        before(0)
-        deal(w2_c[:].bitcast(U16), w2_raw[:].bitcast(U16))
-        before(1)
-        nc.vector.tensor_copy(v_s0[:], tab_s[:].indirect(idx[:]))
-        nc.scalar.dma_start(out=v_s1[0:112, :].bitcast(I32), in_=v_s0[4:116, :].bitcast(I32))
-        pick(0)
-        deal(w2_s[:], w2_sraw[:])
-        pick(1)
-
         w_c = [[keep.tile([P, H], U32, name=f"w_c{i}{a}", align_bytes=64) for a in range(PASSES)] for i in range(2)]
         w_s = [[keep.tile([P, H], U8, name=f"w_s{i}{a}", align_bytes=64) for a in range(PASSES)] for i in range(2)]
 
@@ -163,10 +152,22 @@ def tile_list_free_span_features_kernel(
             for a in range(PASSES):
                 nc.vector.quantize_mx(out=w_c[i][a][:].bitcast(FP8X4), scales=w_s[i][a][:], in_=woven[a][:])
 
+        deal(w2_c[:].bitcast(U16), w2_raw[:].bitcast(U16))
+        deal(w4_c[:].bitcast(U16), w4_raw[:].rearrange("p (g c) -> p g c", g=GROUPS).bitcast(U16))
+        deal(w2_s[:], w2_sraw[:])
+        before(0)
+        before(1)
+        nc.vector.tensor_copy(v_s0[:], tab_s[:].indirect(idx[:]))
+        nc.scalar.dma_start(out=v_s1[0:112, :].bitcast(I32), in_=v_s0[16:128, :].bitcast(I32))
+        pick(0)
+        deal(w4_s[:], w4_sraw[:].rearrange("p (g c) -> p g c", g=GROUPS))
+        quantize_w(0, nc.scalar.copy)
+        pick(1)
+
         h = [keep.tile([P, S], F32, name=f"h{t}") for t in range(PACK)]
 
-        def project(codes, scales, u):
-            acc = psum.tile([P, BANK], F32, name="acc")
+        def project(codes, scales, u, bank):
+            acc = psum.tile([P, BANK], F32, name="acc", tag=f"bank{bank % BANKS}")
             cols = slice(u * BANK, (u + 1) * BANK)
             for a in range(PASSES):
                 nc.tensor.matmul_mx(
@@ -176,26 +177,25 @@ def tile_list_free_span_features_kernel(
                 )
             return acc
 
-        def project_fp8(i, t, u):
+        def project_fp8(i, t, u, bank):
             rows = slice(t * P, (t + 1) * P)
             return project(
                 [w_c[i][a][:, rows].bitcast(FP8X4) for a in range(PASSES)],
-                [w_s[i][a][:, rows] for a in range(PASSES)], u,
+                [w_s[i][a][:, rows] for a in range(PASSES)], u, bank,
             )
 
         for t in range(PACK):
             for u in range(HALVES):
                 acc = project(
                     [w2_c[:, a, 2 * t * P : 2 * (t + 1) * P].bitcast(FP4X4) for a in range(PASSES)],
-                    [w2_s[:, a, t * P : (t + 1) * P] for a in range(PASSES)], u,
+                    [w2_s[:, a, t * P : (t + 1) * P] for a in range(PASSES)], u, HALVES * t + u,
                 )
                 nc.scalar.copy(h[t][:, u * BANK : (u + 1) * BANK], acc[:])
 
-        quantize_w(0, nc.vector.tensor_copy)
         before(2)
         for t in range(PACK):
             for u in range(HALVES):
-                acc = project_fp8(0, t, u)
+                acc = project_fp8(0, t, u, HALVES * t + u)
                 part = h[t][:, u * BANK : (u + 1) * BANK]
                 nc.vector.tensor_tensor(part, acc[:], part, ALU.max)
 
@@ -204,7 +204,7 @@ def tile_list_free_span_features_kernel(
 
         def limit(t):
             for u in range(HALVES):
-                acc = project_fp8(1, t, u)
+                acc = project_fp8(1, t, u, HALVES * (t - 1) + u)
                 part = h[t][:, u * BANK : (u + 1) * BANK]
                 nc.vector.tensor_tensor(part, acc[:], part, ALU.min)
 
@@ -217,8 +217,6 @@ def tile_list_free_span_features_kernel(
         limit(2)
         rewrite(1)
         limit(3)
-        deal(w4_c[:].bitcast(U16), w4_raw[:].rearrange("p (g c) -> p g c", g=GROUPS).bitcast(U16))
-        deal(w4_s[:], w4_sraw[:].rearrange("p (g c) -> p g c", g=GROUPS))
         rewrite(2)
         rewrite(3)
 
@@ -231,8 +229,8 @@ def tile_list_free_span_features_kernel(
 
         def weave(copy, dst, src):
             copy(
-                dst.rearrange("p (c i t) -> p c t i", i=4, t=PACK),
-                src.rearrange("p t (c i) -> p c t i", i=4),
+                dst.rearrange("p (m t) -> p m t", t=PACK),
+                src.rearrange("p t m -> p m t"),
             )
 
         def fetch(m0, m1):
@@ -252,7 +250,8 @@ def tile_list_free_span_features_kernel(
             nc.vector.quantize_mx(out=x_c[:].bitcast(FP8X4), scales=x_s[:], in_=x_b[:])
             for g in range(GROUPS):
                 for b0 in range(0, width, BLOCK):
-                    acc = psum.tile([P, BANK], F32, name="acc")
+                    bank = (GROUPS * m0 + g * width + b0) // BLOCK % BANKS
+                    acc = psum.tile([P, BANK], F32, name="acc", tag=f"bank{bank}")
                     cols = slice(b0, b0 + BLOCK)
                     for t in range(PACK):
                         nc.tensor.matmul_mx(
@@ -290,7 +289,7 @@ def tile_list_free_span_features_kernel(
         for span in spans[1:]:
             finish(*span, nc.vector.tensor_copy)
 
-        for q in range(QUADS):
+        for q in QUAD_ORDER:
             nc.scalar.dma_start(
                 out=out_2[:, 4 * q : 4 * q + 4, :].rearrange("g r m -> r g m").bitcast(I32),
                 in_=y_s[32 * q : 32 * q + 4, :, :].bitcast(I32),

@@ -100,9 +100,9 @@ def tile_list_free_span_features_kernel(
                 out=w4_sraw[32 * q : 32 * q + 4, :].bitcast(I32),
                 in_=w4_scales[0, 4 * q : 4 * q + 4, :].bitcast(I32),
             )
-        for a in range(PASSES):
-            load_w(0, w1, a)
+        load_w(0, w1, 0)
         load_tab(1)
+        load_w(0, w1, 1)
         load_page(2)
         for a in range(PASSES):
             load_w(1, w3, a)
@@ -140,17 +140,13 @@ def tile_list_free_span_features_kernel(
         w_c = [[keep.tile([P, H], U32, name=f"w_c{i}{a}", align_bytes=64) for a in range(PASSES)] for i in range(2)]
         w_s = [[keep.tile([P, H], U8, name=f"w_s{i}{a}", align_bytes=64) for a in range(PASSES)] for i in range(2)]
 
-        def quantize_w(i, copy):
-            woven = []
-            for a in range(PASSES):
-                w_b = ring.tile([P, PACK * H], BF16, name="w_b", align_bytes=64)
-                copy(
-                    w_b[:].rearrange("p (t q j) -> p q t j", t=PACK, j=PACK),
-                    w_raw[i][a][:].rearrange("p j (q t) -> p q t j", t=PACK),
-                )
-                woven.append(w_b)
-            for a in range(PASSES):
-                nc.vector.quantize_mx(out=w_c[i][a][:].bitcast(FP8X4), scales=w_s[i][a][:], in_=woven[a][:])
+        def quantize_w(i, a, copy):
+            w_b = ring.tile([P, PACK * H], BF16, name="w_b", align_bytes=64)
+            copy(
+                w_b[:].rearrange("p (t q j) -> p q t j", t=PACK, j=PACK),
+                w_raw[i][a][:].rearrange("p j (q t) -> p q t j", t=PACK),
+            )
+            nc.vector.quantize_mx(out=w_c[i][a][:].bitcast(FP8X4), scales=w_s[i][a][:], in_=w_b[:])
 
         deal(w2_c[:].bitcast(U16), w2_raw[:].bitcast(U16))
         deal(w4_c[:].bitcast(U16), w4_raw[:].rearrange("p (g c) -> p g c", g=GROUPS).bitcast(U16))
@@ -161,8 +157,9 @@ def tile_list_free_span_features_kernel(
         nc.scalar.dma_start(out=v_s1[0:112, :].bitcast(I32), in_=v_s0[16:128, :].bitcast(I32))
         pick(0)
         deal(w4_s[:], w4_sraw[:].rearrange("p (g c) -> p g c", g=GROUPS))
-        quantize_w(0, nc.scalar.copy)
+        quantize_w(0, 0, nc.scalar.copy)
         pick(1)
+        quantize_w(0, 1, nc.vector.tensor_copy)
 
         h = [keep.tile([P, S], F32, name=f"h{t}") for t in range(PACK)]
 
@@ -199,7 +196,8 @@ def tile_list_free_span_features_kernel(
                 part = h[t][:, u * BANK : (u + 1) * BANK]
                 nc.vector.tensor_tensor(part, acc[:], part, ALU.max)
 
-        quantize_w(1, nc.scalar.copy)
+        quantize_w(1, 0, nc.scalar.copy)
+        quantize_w(1, 1, nc.scalar.copy)
         before(3)
 
         def limit(t):

from contextlib import ExitStack

import concourse.mybir as mybir

K, T, S, T2, M, H, N = 1024, 4096, 1024, 2048, 1024, 512, 1024
FLOPS = 2 * (3 * K * H * S + H * N * M)

F32 = mybir.dt.float32
BF16 = mybir.dt.bfloat16
I32 = mybir.dt.int32
U32 = mybir.dt.uint32
U16 = mybir.dt.uint16
U8 = mybir.dt.uint8
FP8X4 = mybir.dt.float8_e4m3fn_x4
FP4X4 = mybir.dt.float4_e2m1fn_x4
ALU = mybir.AluOpType
ACT = mybir.ActivationFunctionType

P = 128
PACK = 4
PASSES = K // (P * PACK)
GROUPS = N // (P * PACK)
BANK = 512
HALVES = S // BANK
EDGES = (0, 128, 384, 640, 896, 1024)
BLOCK = 128
BANKS = 8
QUAD_ORDER = (0, 2, 1, 3)


def tile_list_free_span_features_kernel(
    tc, tab_words, tab_scales, offs, offs2, offs3, offs4, w1, w2_words, w2_scales, w3, wgs, page0, shift,
    w4_words, w4_scales, out_0, out_1, out_2,
):
    nc = tc.nc
    with ExitStack() as ctx:
        lists = ctx.enter_context(tc.tile_pool(name="lists", bufs=1))
        keep = ctx.enter_context(tc.tile_pool(name="keep", bufs=1))
        ring = ctx.enter_context(tc.tile_pool(name="ring", bufs=2))
        psum = ctx.enter_context(tc.psum_pool(name="psum", bufs=1))

        idx = lists.tile([P, S // 16], U16, name="idx")
        idx2 = lists.tile([P, S // 16], U16, name="idx2")
        idx3 = lists.tile([P, M // 16], U16, name="idx3")
        idx4 = lists.tile([P, M // 16], U16, name="idx4")

        tab_w = [keep.tile([P, T], I32, name=f"tab_w{a}", tag=f"big{a}", align_bytes=64) for a in range(PASSES)]
        tab_s = keep.tile([P, T], U8, name="tab_s")
        page = [keep.tile([P, T2], F32, name=f"page{t}") for t in range(PACK)]
        gain = keep.tile([P, PACK, S], F32, name="gain", tag="gain")
        w_raw = [[keep.tile([P, PACK, H], F32, name=f"w_raw{i}{a}") for a in range(PASSES)] for i in range(2)]
        w2_raw = keep.tile([P, PASSES, 2 * H], U8, name="w2_raw")
        w2_sraw = keep.tile([P, PASSES, H], U8, name="w2_sraw")
        w4_raw = keep.tile([P, 2 * N], U8, name="w4_raw")
        w4_sraw = keep.tile([P, N], U8, name="w4_sraw")
        shift_t = keep.tile([P, PACK], F32, name="shift_t")
        v_s1 = keep.tile([P, S], U8, name="v_s1", align_bytes=64)

        page_rows = page0.rearrange("(p t) c -> t p c", t=PACK)
        gain_rows = wgs.rearrange("(p t) j -> p t j", t=PACK)

        def load_w(i, w, a):
            rows = w[a * P * PACK : (a + 1) * P * PACK, :]
            nc.sync.dma_start(out=w_raw[i][a][:], in_=rows.rearrange("(p j) c -> p j c", j=PACK))

        def load_tab(a):
            nc.sync.dma_start(out=tab_w[a][:], in_=tab_words[a].rearrange("p c i -> p (c i)").bitcast(I32))

        nc.vector.memset(w2_sraw[:].rearrange("p a c -> p (a c)").bitcast(I32), 0)
        nc.vector.memset(tab_s[:].bitcast(I32), 0)
        nc.vector.memset(w4_sraw[:].bitcast(I32), 0)
        nc.vector.memset(v_s1[:].bitcast(I32), 0)

        def load_page(t):
            nc.sync.dma_start(out=page[t][:], in_=page_rows[t])

        def load_w2_scales(q):
            nc.sync.dma_start(
                out=w2_sraw[32 * q : 32 * q + 4, :, :].bitcast(I32),
                in_=w2_scales[:, 4 * q : 4 * q + 4, :].rearrange("a r c -> r a c").bitcast(I32),
            )

        nc.sync.dma_start(out=w2_raw[:].bitcast(I32), in_=w2_words.rearrange("a p c -> p a c").bitcast(I32))
        nc.sync.dma_start(out=w4_raw[:].bitcast(I32), in_=w4_words[0].bitcast(I32))
        nc.sync.dma_start(idx4[:], offs4)
        nc.sync.dma_start(idx[:], offs)
        nc.sync.dma_start(out=shift_t[:], in_=shift.rearrange("(p t) -> p t", t=PACK))
        nc.sync.dma_start(idx2[:], offs2)
        nc.sync.dma_start(idx3[:], offs3)
        load_page(0)
        for q in QUAD_ORDER:
            load_w2_scales(q)
        load_page(1)
        tab_rows = tab_scales.rearrange("a (q r) c -> r q a c", r=4).bitcast(I32)
        for r in range(4):
            nc.sync.dma_start(out=tab_s[r:P:16, :].bitcast(I32), in_=tab_rows[r])
        load_tab(0)
        for q in QUAD_ORDER:
            nc.sync.dma_start(
                out=w4_sraw[32 * q : 32 * q + 4, :].bitcast(I32),
                in_=w4_scales[0, 4 * q : 4 * q + 4, :].bitcast(I32),
            )
        load_w(0, w1, 0)
        load_tab(1)
        load_w(0, w1, 1)
        load_page(2)
        for a in range(PASSES):
            load_w(1, w3, a)
        load_page(3)
        for q in QUAD_ORDER:
            nc.sync.dma_start(out=gain[32 * q : 32 * q + 32, 0, :], in_=gain_rows[:, 0, :])
        for q in QUAD_ORDER:
            nc.sync.dma_start(out=gain[32 * q : 32 * q + 32, 1:PACK, :], in_=gain_rows[:, 1:PACK, :])

        v_s0 = keep.tile([P, S], U8, name="v_s0", align_bytes=64)
        v_s = [v_s0, v_s1]

        base = [keep.tile([P, M], F32, name=f"base{t}") for t in range(PACK)]

        def before(t):
            old = ring.tile([P, M], F32, name="old")
            nc.vector.tensor_copy(old[:], page[t][:].indirect(idx4[:]))
            nc.scalar.activation(base[t][:], old[:], ACT.Identity, bias=shift_t[:, t : t + 1], scale=-1.0)

        v_w = [keep.tile([P, S], U32, name=f"v_w{a}", align_bytes=64) for a in range(PASSES)]

        def pick(a):
            nc.vector.tensor_copy(v_w[a][:], tab_w[a][:].bitcast(U32).indirect(idx[:]))

        w2_c = keep.tile([P, PASSES, 2 * H], U8, name="w2_c", align_bytes=64)
        w2_s = keep.tile([P, PASSES, H], U8, name="w2_s", align_bytes=64)
        w4_c = keep.tile([P, GROUPS, 2 * BANK], U8, name="w4_c", align_bytes=64)
        w4_s = keep.tile([P, GROUPS, BANK], U8, name="w4_s", align_bytes=64)

        def deal(dst, src):
            nc.vector.tensor_copy(
                dst.rearrange("p a (t q) -> p a t q", t=PACK), src.rearrange("p a (q t) -> p a t q", t=PACK)
            )

        w_c = [[keep.tile([P, H], U32, name=f"w_c{i}{a}", align_bytes=64) for a in range(PASSES)] for i in range(2)]
        w_s = [[keep.tile([P, H], U8, name=f"w_s{i}{a}", align_bytes=64) for a in range(PASSES)] for i in range(2)]

        def quantize_w(i, a, copy):
            w_b = ring.tile([P, PACK * H], BF16, name="w_b", align_bytes=64)
            copy(
                w_b[:].rearrange("p (t q j) -> p q t j", t=PACK, j=PACK),
                w_raw[i][a][:].rearrange("p j (q t) -> p q t j", t=PACK),
            )
            nc.vector.quantize_mx(out=w_c[i][a][:].bitcast(FP8X4), scales=w_s[i][a][:], in_=w_b[:])

        deal(w2_c[:].bitcast(U16), w2_raw[:].bitcast(U16))
        deal(w4_c[:].bitcast(U16), w4_raw[:].rearrange("p (g c) -> p g c", g=GROUPS).bitcast(U16))
        deal(w2_s[:], w2_sraw[:])
        before(0)
        before(1)
        nc.vector.tensor_copy(v_s0[:], tab_s[:].indirect(idx[:]))
        nc.scalar.dma_start(out=v_s1[0:112, :].bitcast(I32), in_=v_s0[16:128, :].bitcast(I32))
        pick(0)
        deal(w4_s[:], w4_sraw[:].rearrange("p (g c) -> p g c", g=GROUPS))
        quantize_w(0, 0, nc.scalar.copy)
        pick(1)
        quantize_w(0, 1, nc.vector.tensor_copy)

        h = [keep.tile([P, S], F32, name=f"h{t}") for t in range(PACK)]

        def project(codes, scales, u, bank):
            acc = psum.tile([P, BANK], F32, name="acc", tag=f"bank{bank % BANKS}")
            cols = slice(u * BANK, (u + 1) * BANK)
            for a in range(PASSES):
                nc.tensor.matmul_mx(
                    out=acc[:], lhsT=codes[a], lhsT_scale=scales[a],
                    rhs=v_w[a][:, cols].bitcast(FP8X4), rhs_scale=v_s[a][:, cols],
                    start=(a == 0), stop=(a == PASSES - 1),
                )
            return acc

        def project_fp8(i, t, u, bank):
            rows = slice(t * P, (t + 1) * P)
            return project(
                [w_c[i][a][:, rows].bitcast(FP8X4) for a in range(PASSES)],
                [w_s[i][a][:, rows] for a in range(PASSES)], u, bank,
            )

        for t in range(PACK):
            for u in range(HALVES):
                acc = project(
                    [w2_c[:, a, 2 * t * P : 2 * (t + 1) * P].bitcast(FP4X4) for a in range(PASSES)],
                    [w2_s[:, a, t * P : (t + 1) * P] for a in range(PASSES)], u, HALVES * t + u,
                )
                nc.scalar.copy(h[t][:, u * BANK : (u + 1) * BANK], acc[:])

        before(2)
        for t in range(PACK):
            for u in range(HALVES):
                acc = project_fp8(0, t, u, HALVES * t + u)
                part = h[t][:, u * BANK : (u + 1) * BANK]
                nc.vector.tensor_tensor(part, acc[:], part, ALU.max)

        quantize_w(1, 0, nc.scalar.copy)
        quantize_w(1, 1, nc.scalar.copy)
        before(3)

        def limit(t):
            for u in range(HALVES):
                acc = project_fp8(1, t, u, HALVES * (t - 1) + u)
                part = h[t][:, u * BANK : (u + 1) * BANK]
                nc.vector.tensor_tensor(part, acc[:], part, ALU.min)

        def rewrite(t):
            nc.vector.tensor_tensor(page[t][:].indirect(idx2[:]), h[t][:], gain[:, t, :], ALU.mult)

        limit(0)
        limit(1)
        rewrite(0)
        limit(2)
        rewrite(1)
        limit(3)
        rewrite(2)
        rewrite(3)

        x_f = keep.tile([P, PACK * M], F32, name="x_f", tag="gain")
        y = [keep.tile([P, PACK, M], F32, name=f"y{g}", tag=f"big{g}", align_bytes=64) for g in range(GROUPS)]
        y_c = keep.tile([P, GROUPS, M], I32, name="y_c", align_bytes=64)
        y_s = keep.tile([P, GROUPS, M], U8, name="y_s", align_bytes=64)
        y_rows = out_0.rearrange("(g p t) m -> g p t m", p=P, t=PACK)
        y_words = out_1.rearrange("g p m t -> p g (m t)").bitcast(I32)

        def weave(copy, dst, src):
            copy(
                dst.rearrange("p (m t) -> p m t", t=PACK),
                src.rearrange("p t m -> p m t"),
            )

        def fetch(m0, m1):
            width = m1 - m0
            part = idx3[:, m0 // 16 : m1 // 16]
            x_part = x_f[:, PACK * m0 : PACK * m1].rearrange("p (t m) -> p t m", t=PACK)
            for t in range(PACK):
                nc.vector.tensor_tensor(x_part[:, t, :], page[t][:].indirect(part), base[t][:, m0:m1], ALU.add)
            x_b = ring.tile([P, PACK * width], BF16, name="x_b", align_bytes=64)
            weave(nc.scalar.copy, x_b[:], x_part)
            return x_b

        def multiply(m0, m1, x_b):
            width = m1 - m0
            x_c = ring.tile([P, width], U32, name="x_c", align_bytes=64)
            x_s = ring.tile([P, width], U8, name="x_s", align_bytes=64)
            nc.vector.quantize_mx(out=x_c[:].bitcast(FP8X4), scales=x_s[:], in_=x_b[:])
            for g in range(GROUPS):
                for b0 in range(0, width, BLOCK):
                    bank = (GROUPS * m0 + g * width + b0) // BLOCK % BANKS
                    acc = psum.tile([P, BANK], F32, name="acc", tag=f"bank{bank}")
                    cols = slice(b0, b0 + BLOCK)
                    for t in range(PACK):
                        nc.tensor.matmul_mx(
                            out=acc[:, t * BLOCK : (t + 1) * BLOCK],
                            lhsT=w4_c[:, g, 2 * t * P : 2 * (t + 1) * P].bitcast(FP4X4),
                            lhsT_scale=w4_s[:, g, t * P : (t + 1) * P],
                            rhs=x_c[:, cols].bitcast(FP8X4), rhs_scale=x_s[:, cols],
                            start=True, stop=True,
                        )
                    nc.scalar.copy(
                        y[g][:, :, m0 + b0 : m0 + b0 + BLOCK], acc[:].rearrange("p (t m) -> p t m", t=PACK)
                    )

        def finish(m0, m1, copy):
            cols = slice(m0, m1)
            woven = []
            for g in range(GROUPS):
                nc.sync.dma_start(out=y_rows[g][:, :, cols], in_=y[g][:, :, cols])
                y_b = ring.tile([P, PACK * (m1 - m0)], BF16, name="y_b", bufs=4, align_bytes=64)
                weave(copy, y_b[:], y[g][:, :, cols])
                woven.append(y_b)
            for g in range(GROUPS):
                nc.vector.quantize_mx(out=y_c[:, g, cols].bitcast(FP8X4), scales=y_s[:, g, cols], in_=woven[g][:])
            nc.sync.dma_start(out=y_words[:, :, cols], in_=y_c[:, :, cols])

        spans = list(zip(EDGES[:-1], EDGES[1:]))
        x_next = fetch(*spans[0])
        for c, span in enumerate(spans):
            x_b = x_next
            if c + 1 < len(spans):
                x_next = fetch(*spans[c + 1])
            multiply(*span, x_b)
            if c == 0:
                finish(*span, nc.scalar.copy)
        for span in spans[1:]:
            finish(*span, nc.vector.tensor_copy)

        for q in QUAD_ORDER:
            nc.scalar.dma_start(
                out=out_2[:, 4 * q : 4 * q + 4, :].rearrange("g r m -> r g m").bitcast(I32),
                in_=y_s[32 * q : 32 * q + 4, :, :].bitcast(I32),
            )
